import numpy as np
import ml_dtypes


def mxq(x, axis, fmt="e4m3"):
    dtype, down = {"e4m3": (ml_dtypes.float8_e4m3fn, 7), "e5m2": (ml_dtypes.float8_e5m2, 14)}[fmt]
    v = np.moveaxis(np.asarray(x, np.float32).astype(ml_dtypes.bfloat16).astype(np.float64), axis, -1)
    blocks = v.reshape(v.shape[:-1] + (-1, 32))
    amax = np.abs(blocks).max(-1, keepdims=True)
    byte = np.maximum(np.where(amax > 0, np.frexp(amax)[1] - 1 + 127, 0) - down, 1)
    scale = np.exp2(byte - 127.0)
    codes = (blocks / scale).astype(np.float32).astype(dtype).astype(np.float64)
    return np.moveaxis((codes * scale).reshape(v.shape), -1, axis)


WIDE = False


def mx_kscale(k):
    if not WIDE:
        return np.ones(k)
    levels = np.array([10, -10, 5, -5, 0])
    if k % 512:
        return np.exp2(np.random.permutation(np.resize(levels, k // 32))).repeat(32)
    a = np.empty((k // 512, 16))
    for p in range(k // 512):
        a[p, :8] = np.random.permutation(np.resize(levels, 8))
        for g in range(8):
            far = levels[np.abs(levels - a[p, g]) >= 10]
            a[p, g + 8] = far[np.random.randint(len(far))]
    return np.exp2(a.ravel()).repeat(32)


def f64(x):
    return np.asarray(x).astype(np.float64)


def striped(idx):
    return np.tile(idx.reshape(-1, 16).T, (8, 1)).astype(np.uint16)


def unstriped(offs):
    return offs[:16].T.reshape(-1).astype(np.int64)


E2M1 = np.array([0.0, 0.5, 1.0, 1.5, 2.0, 3.0, 4.0, 6.0, -0.0, -0.5, -1.0, -1.5, -2.0, -3.0, -4.0, -6.0])


def pack_weight(w, fmt):
    k, n = w.shape
    w = f64(np.asarray(w, np.float32).astype(ml_dtypes.bfloat16)).reshape(k // 32, 32, n)
    amax = np.abs(w).max(1)
    if fmt == "e4m3":
        byte = np.frexp(amax)[1] - 1 + 127 - 7
    else:
        mant, ex = np.frexp(amax / 6.0)
        byte = np.where(mant > 0.5, ex, ex - 1) + 127
    byte = np.clip(np.where(amax > 0, byte, 1), 1, 254)
    scaled = (w * np.exp2(127.0 - byte)[:, None, :]).reshape(k, n).astype(np.float32)
    by_word = np.ascontiguousarray(scaled.reshape(k // 512, 128, 4, n).transpose(0, 1, 3, 2))
    if fmt == "e4m3":
        words = by_word.astype(ml_dtypes.float8_e4m3fn).view(np.uint8)
    else:
        c = by_word.astype(ml_dtypes.float4_e2m1fn).view(np.uint8) & 0xF
        words = (c[..., 0::2] | (c[..., 1::2] << 4)).reshape(k // 512, 128, 2 * n)
    return np.ascontiguousarray(words), np.ascontiguousarray(byte.astype(np.uint8).reshape(k // 512, 16, n))


def unpack_weight(words, scales, fmt):
    g, _, n = scales.shape
    words = np.ascontiguousarray(words).reshape(g, 128, n, -1)
    if fmt == "e4m3":
        vals = words.view(ml_dtypes.float8_e4m3fn).astype(np.float64)
    else:
        nib = np.empty((g, 128, n, 4), np.uint8)
        nib[..., 0::2] = words & 0xF
        nib[..., 1::2] = words >> 4
        vals = E2M1[nib]
    vals = vals * np.repeat(np.exp2(scales.astype(np.float64) - 127.0), 8, axis=1)[..., None]
    return vals.transpose(0, 1, 3, 2).reshape(g * 512, n)


def gelu(v):
    return 0.5 * v * (1.0 + np.tanh(np.sqrt(2.0 / np.pi) * (v + 0.044715 * v**3)))


K, T, S, H, T2, P = 1536, 2048, 512, 1024, 1024, 512

def setup_inputs():
    n = np.random.standard_normal
    s = mx_kscale(K)[:, None]
    u = mx_kscale(H)[:, None]
    d = {}
    d["tab_words"], d["tab_scales"] = pack_weight(n((K, T)) * s, "e4m3")
    d["offs"] = striped(np.random.permutation(T)[:S])
    d["w1"] = (n((K, H)) / K**0.5 / s * u.T).astype(np.float32)
    d["resid"] = (0.7 * n((H, S)) * u).astype(np.float32)
    d["page0"] = (n((H, T2)) * u).astype(np.float32)
    d["wgs"] = np.exp(0.3 * n((128, S))).astype(np.float32)
    d["offs2"] = striped(np.random.permutation(T2)[:S])
    d["offs3"] = striped(np.random.permutation(T2)[:P])
    d["w4_words"], d["w4_scales"] = pack_weight(n((H, H)) / H**0.5 / u * u.T, "e2m1")
    d["least"] = (0.6 * n(H) * u[:, 0]).astype(np.float32)
    d["gain"] = (np.exp(0.4 * n(H)) / H**0.5 / u[:, 0]**2).astype(np.float32)
    d["slot"] = (0.8 * n(T2)).astype(np.float32)
    return d

def reference(tab_words, tab_scales, offs, w1, resid, page0, wgs, offs2, offs3, w4_words, w4_scales, least, gain, slot):
    v = unpack_weight(tab_words, tab_scales, "e4m3")[:, unstriped(offs)]
    h = (mxq(f64(w1), 0, "e4m3").T @ v) + f64(resid)
    page = f64(page0).copy()
    page[:, unstriped(offs2)] = np.tile(f64(wgs), (H // 128, 1)) * h
    x = page[:, unstriped(offs3)]
    w4 = unpack_weight(w4_words, w4_scales, "e2m1")
    y = w4.T @ mxq(x, 0, "e4m3")
    z = np.maximum(y, f64(least)[:, None]) * f64(gain)[:, None]
    e = mxq(page, 0, "e4m3").T @ mxq(z, 0, "e4m3")
    return e + f64(slot)[:, None]

@@ -1,0 +1,375 @@
+from contextlib import ExitStack
+
+import concourse.mybir as mybir
+
+K, T, S, H, T2, NP = 1536, 2048, 512, 1024, 1024, 512
+FLOPS = 2 * K * H * S + 2 * H * H * NP + 2 * H * T2 * NP
+
+F32 = mybir.dt.float32
+BF16 = mybir.dt.bfloat16
+I32 = mybir.dt.int32
+U32 = mybir.dt.uint32
+U16 = mybir.dt.uint16
+U8 = mybir.dt.uint8
+FP8X4 = mybir.dt.float8_e4m3fn_x4
+FP4X4 = mybir.dt.float4_e2m1fn_x4
+ALU = mybir.AluOpType
+ACT = mybir.ActivationFunctionType
+
+P = 128
+PACK = 4
+KP = P * PACK
+KA = K // KP
+RB = H // KP
+HALF = NP // 2
+
+
+def tile_list_canteen_menu_rotation_kernel(
+    tc, tab_words, tab_scales, offs, w1, resid, page0, wgs, offs2, offs3, w4_words, w4_scales, least, gain, slot, out
+):
+    nc = tc.nc
+    with ExitStack() as ctx:
+        keep = ctx.enter_context(tc.tile_pool(name="keep", bufs=1))
+        ring = ctx.enter_context(tc.tile_pool(name="ring", bufs=1))
+        psum = ctx.enter_context(tc.psum_pool(name="psum", bufs=1))
+
+        def held(name, shape, dtype):
+            return keep.tile(shape, dtype, name=name, align_bytes=64)
+
+        def slab(name, shape, dtype):
+            return ring.tile(shape, dtype, name=name, tag="slab", bufs=7, align_bytes=64)
+
+        def bank(name, tag):
+            return psum.tile([P, 512], F32, name=name, tag=tag, bufs=4)
+
+        idx = held("idx", [P, S // 16], U16)
+        idx2 = held("idx2", [P, S // 16], U16)
+        idx3 = held("idx3", [P, NP // 16], U16)
+
+        tab_sc = held("tab_sc", [P, T], U8)
+        w4_raw = held("w4_raw", [P, RB, 2 * H], U8)
+        w4_sc_raw = held("w4_sc_raw", [P, RB, H], U8)
+        nc.gpsimd.memset(tab_sc[:].bitcast(I32), 0)
+        nc.gpsimd.memset(w4_sc_raw[:].rearrange("p a n -> p (a n)").bitcast(I32), 0)
+
+        def load_w1(b, a):
+            if (b, a) == (RB - 1, KA - 1):
+                raw = ring.tile([P, PACK, KP], F32, name="w1_raw_last", tag="last_raw", bufs=1, align_bytes=64)
+            else:
+                raw = slab("w1_raw_%d_%d" % (b, a), [P, PACK, KP], F32)
+            src = w1[a * KP : (a + 1) * KP, b * KP : (b + 1) * KP].rearrange("(p i) c -> p i c", i=PACK)
+            nc.sync.dma_start(out=raw[:], in_=src)
+            return raw
+
+        def load_tab(a):
+            words = slab("tab_%d" % a, [P, T], I32)
+            nc.sync.dma_start(out=words[:], in_=tab_words[a].rearrange("p t i -> p (t i)").bitcast(I32))
+            return words
+
+        resid_rows = resid.rearrange("(b p t) j -> b t p j", b=RB, t=PACK)
+        page_rows = page0.rearrange("(b p t) m -> b t p m", b=RB, t=PACK)
+        res = [held("res_%d" % i, [P, S], F32) for i in range(RB * PACK)]
+        page = [held("page_%d" % i, [P, T2], F32) for i in range(RB * PACK)]
+
+        def load_res(i):
+            nc.sync.dma_start(out=res[i][:], in_=resid_rows[i // PACK, i % PACK])
+
+        def load_page(i):
+            nc.sync.dma_start(out=page[i][:], in_=page_rows[i // PACK, i % PACK])
+
+        nc.sync.dma_start(out=w4_raw[:].bitcast(I32), in_=w4_words.rearrange("a p c -> p a c").bitcast(I32))
+        w1_raw = {}
+        tab = []
+        w1_raw[0, 0] = load_w1(0, 0)
+        tab.append(load_tab(0))
+        nc.sync.dma_start(idx[:], offs)
+        for q in range(4):
+            nc.scalar.dma_start(
+                out=tab_sc[32 * q : 32 * q + 4 * KA, :].bitcast(I32),
+                in_=tab_scales[:, 4 * q : 4 * q + 4, :].bitcast(I32),
+            )
+        w1_raw[0, 1] = load_w1(0, 1)
+        tab.append(load_tab(1))
+        w1_raw[0, 2] = load_w1(0, 2)
+        for q in range(4):
+            nc.scalar.dma_start(
+                out=w4_sc_raw[32 * q : 32 * q + 4, :, :].bitcast(I32),
+                in_=w4_scales[:, 4 * q : 4 * q + 4, :].rearrange("a r n -> r a n").bitcast(I32),
+            )
+        wg_first = held("wg_first", [P, S], F32)
+        wg_rest = held("wg_rest", [P, PACK - 1, S], F32)
+        wg_rows = wgs.rearrange("(q t) j -> q t j", t=PACK)
+        tab.append(load_tab(2))
+        load_res(0)
+        for q in range(4):
+            nc.sync.dma_start(out=wg_first[32 * q : 32 * q + 32, :], in_=wg_rows[:, 0, :])
+        nc.sync.dma_start(idx2[:], offs2)
+        load_page(0)
+        load_res(1)
+        nc.sync.dma_start(idx3[:], offs3)
+        for q in range(4):
+            nc.sync.dma_start(out=wg_rest[32 * q : 32 * q + 32, :, :], in_=wg_rows[:, 1:PACK, :])
+        load_page(1)
+        load_res(2)
+        w1_raw[1, 0] = load_w1(1, 0)
+        w1_raw[1, 1] = load_w1(1, 1)
+        load_page(2)
+        load_res(3)
+        w1_raw[1, 2] = load_w1(1, 2)
+        load_page(3)
+        for i in range(PACK, RB * PACK):
+            load_res(i)
+        for i in range(PACK + 1, RB * PACK):
+            load_page(i)
+        load_page(PACK)
+        least_sb = held("least_sb", [P, RB, PACK], F32)
+        gain_sb = held("gain_sb", [P, RB, PACK], F32)
+        slot_sb = held("slot_sb", [P, T2 // P], F32)
+        nc.sync.dma_start(out=least_sb[:], in_=least.rearrange("(b p t) -> p b t", b=RB, t=PACK))
+        nc.sync.dma_start(out=gain_sb[:], in_=gain.rearrange("(b p t) -> p b t", b=RB, t=PACK))
+        with nc.allow_non_contiguous_dma(reason="one value of slot to a partition"):
+            nc.sync.dma_start(out=slot_sb[:], in_=slot.rearrange("(c p) -> p c", p=P))
+
+        def wg(t):
+            return wg_first[:] if t == 0 else wg_rest[:, t - 1, :]
+
+        w4 = held("w4", [P, RB, 2 * H], U8)
+        w4_sc = held("w4_sc", [P, RB, H], U8)
+        for a in range(RB):
+            nc.vector.tensor_copy(
+                out=w4[:, a, :].rearrange("p (b t m e) -> p b t m e", b=RB, t=PACK, e=2),
+                in_=w4_raw[:, a, :].rearrange("p (b m t e) -> p b t m e", b=RB, t=PACK, e=2),
+            )
+        nc.vector.tensor_copy(
+            out=w4_sc[:].rearrange("p a (b t m) -> p (a b) t m", b=RB, t=PACK),
+            in_=w4_sc_raw[:].rearrange("p a (b m t) -> p (a b) t m", b=RB, t=PACK),
+        )
+
+        v_sc = held("v_sc", [P, S], U8)
+        v = [held("v_%d" % a, [P, S], U32) for a in range(KA)]
+        w1_codes = {}
+        w1_sc = {}
+
+        def gather_tab(a):
+            nc.vector.tensor_copy(v[a][:], tab[a][:].bitcast(U32).indirect(idx[:]))
+
+        def quant_w1(b, a, split):
+            if (b, a) == (RB - 1, KA - 1):
+                staged = ring.tile([P, PACK * KP], BF16, name="w1_bf_last", tag="last_bf", bufs=1, align_bytes=64)
+            else:
+                staged = ring.tile(
+                    [P, PACK * KP], BF16, name="w1_bf_%d_%d" % (b, a), tag="w1_bf", bufs=2, align_bytes=64
+                )
+            dst = staged[:].rearrange("p (t m i) -> p m i t", t=PACK, i=PACK)
+            src = w1_raw[b, a][:].rearrange("p i (m t) -> p m i t", t=PACK)
+            if split:
+                nc.scalar.copy(out=dst[:, 0:split], in_=src[:, 0:split])
+                nc.vector.tensor_copy(out=dst[:, split:P], in_=src[:, split:P])
+            else:
+                nc.scalar.copy(out=dst, in_=src)
+            w1_codes[b, a] = held("w1_codes_%d_%d" % (b, a), [P, KP], U32)
+            w1_sc[b, a] = held("w1_sc_%d_%d" % (b, a), [P, KP], U8)
+            nc.vector.quantize_mx(out=w1_codes[b, a][:].bitcast(FP8X4), scales=w1_sc[b, a][:], in_=staged[:])
+
+        nc.vector.tensor_copy(v_sc[:], tab_sc[:].indirect(idx[:]))
+        gather_tab(0)
+        quant_w1(0, 0, 0)
+        gather_tab(1)
+        quant_w1(0, 1, 0)
+        quant_w1(0, 2, 48)
+        gather_tab(2)
+
+        h_bank = {}
+
+        def h_pass(i, a):
+            b, t = divmod(i, PACK)
+            if a == 0:
+                h_bank[i] = bank("h_bank_%d" % i, "a")
+            cols = slice(t * P, (t + 1) * P)
+            nc.tensor.matmul_mx(
+                out=h_bank[i][:],
+                lhsT=w1_codes[b, a][:, cols].bitcast(FP8X4),
+                lhsT_scale=w1_sc[b, a][:, cols],
+                rhs=v[a][:].bitcast(FP8X4),
+                rhs_scale=v_sc[4 * a : P, :],
+                start=(a == 0),
+                stop=(a == KA - 1),
+            )
+
+        for a in range(KA):
+            for i in range(PACK):
+                h_pass(i, a)
+
+        x_planes = [held("x_planes_%d" % b, [P, PACK, NP], BF16) for b in range(RB)]
+        x_codes = [held("x_codes_%d" % b, [P, NP], U32) for b in range(RB)]
+        x_sc = [held("x_sc_%d" % b, [P, NP], U8) for b in range(RB)]
+        pg_codes = [held("pg_codes_%d" % b, [P, T2], U32) for b in range(RB)]
+        pg_sc = [held("pg_sc_%d" % b, [P, T2], U8) for b in range(RB)]
+
+        def woven(name):
+            return ring.tile([P, PACK * HALF], BF16, name=name, tag="woven", bufs=4, align_bytes=64)
+
+        def weave(copy, dst, planes):
+            copy(
+                out=dst[:].rearrange("p (c i t) -> p c t i", i=4, t=PACK),
+                in_=planes.rearrange("p t (c i) -> p c t i", i=4),
+            )
+
+        def quant_x(b, half, copy):
+            cols = slice(half * HALF, (half + 1) * HALF)
+            dst = woven("x_woven_%d_%d" % (b, half))
+            weave(copy, dst, x_planes[b][:, :, cols])
+            nc.vector.quantize_mx(out=x_codes[b][:, cols].bitcast(FP8X4), scales=x_sc[b][:, cols], in_=dst[:])
+
+        def weave_page(b):
+            whole = slab("pg_woven_%d" % b, [P, T2, 2], F32)
+            words = pairs[b][:].rearrange("p u m e -> p u (m e)").bitcast(F32)
+            nc.scalar.copy(out=whole[:], in_=words.rearrange("p u m -> p m u"))
+            return whole
+
+        def quant_page(b, whole):
+            nc.vector.quantize_mx(
+                out=pg_codes[b][:].bitcast(FP8X4),
+                scales=pg_sc[b][:],
+                in_=whole[:].rearrange("p m u -> p (m u)").bitcast(BF16),
+            )
+
+        y_bank = {}
+
+        def y_pass(half, k, a):
+            if a == 0:
+                y_bank[half, k] = bank("y_bank_%d_%d" % (half, k), "b" if half == 0 else "a")
+            for u in range(2):
+                n = 2 * k + u
+                for c in range(2):
+                    cols = slice(half * HALF + c * P, half * HALF + (c + 1) * P)
+                    nc.tensor.matmul_mx(
+                        out=y_bank[half, k][:, u * HALF + c * P : u * HALF + (c + 1) * P],
+                        lhsT=w4[:, a, 2 * P * n : 2 * P * (n + 1)].bitcast(FP4X4),
+                        lhsT_scale=w4_sc[:, a, P * n : P * (n + 1)],
+                        rhs=x_codes[a][:, cols].bitcast(FP8X4),
+                        rhs_scale=x_sc[a][:, cols],
+                        start=(a == 0 and u == 0 and c == 0),
+                        stop=(a == RB - 1 and u == 1 and c == 1),
+                    )
+
+        h = {}
+        pairs = []
+
+        def add_resid(i):
+            if i == PACK - 1:
+                h[i] = ring.tile([P, S], F32, name="h_%d" % i, tag="last_bf", bufs=1, align_bytes=64)
+            else:
+                h[i] = ring.tile([P, S], F32, name="h_%d" % i, tag="h", bufs=2)
+            nc.vector.tensor_tensor(h[i][:], h_bank[i][:], res[i][:], ALU.add)
+
+        add_resid(0)
+        for i in range(RB * PACK):
+            b, t = divmod(i, PACK)
+            nc.vector.tensor_tensor(page[i][:].indirect(idx2[:]), h[i][:], wg(t), ALU.mult)
+            if i < KA:
+                quant_w1(1, i, 0)
+            if i == KA - 1:
+                for a in range(KA):
+                    for i2 in range(PACK, 2 * PACK):
+                        h_pass(i2, a)
+            if i + 1 < RB * PACK:
+                add_resid(i + 1)
+            nc.vector.tensor_copy(x_planes[b][:, t, :], page[i][:].indirect(idx3[:]))
+            if i == RB * PACK - 1:
+                quant_x(b, 0, nc.vector.tensor_copy)
+            if i == PACK:
+                pairs.append(slab("pairs_1", [P, 2, T2, 2], BF16))
+            if i == KA - 1:
+                pairs.append(ring.tile([P, 2, T2, 2], BF16, name="pairs_0", tag="last_raw", bufs=1, align_bytes=64))
+                for i2 in range(i):
+                    nc.scalar.copy(out=pairs[0][:, i2 // 2, :, i2 % 2], in_=page[i2][:])
+            if i >= KA - 1:
+                nc.scalar.copy(out=pairs[b][:, t // 2, :, t % 2], in_=page[i][:])
+            if i == PACK - 1:
+                quant_x(0, 0, nc.scalar.copy)
+                quant_x(0, 1, nc.scalar.copy)
+                quant_page(0, weave_page(0))
+                for k in range(4):
+                    y_pass(0, k, 0)
+        page_woven = weave_page(1)
+        for k in range(4):
+            y_pass(0, k, 1)
+        quant_x(1, 1, nc.scalar.copy)
+        for k in range(4):
+            y_pass(1, k, 0)
+        for k in range(4):
+            y_pass(1, k, 1)
+
+        z_codes = {}
+        z_sc = {}
+
+        def make_z(half, b):
+            planes = ring.tile([P, PACK, HALF], BF16, name="z_planes_%d_%d" % (half, b), tag="z_planes", bufs=4)
+            for t in range(PACK):
+                k, u = divmod(PACK * b + t, 2)
+                nc.vector.tensor_scalar(
+                    planes[:, t, :],
+                    y_bank[half, k][:, u * HALF : (u + 1) * HALF],
+                    least_sb[:, b, t : t + 1],
+                    gain_sb[:, b, t : t + 1],
+                    ALU.max,
+                    ALU.mult,
+                )
+            return planes
+
+        def quant_z(half, b, planes, copy):
+            dst = woven("z_woven_%d_%d" % (half, b))
+            weave(copy, dst, planes[:])
+            z_codes[half, b] = held("z_codes_%d_%d" % (half, b), [P, HALF], U32)
+            z_sc[half, b] = held("z_sc_%d_%d" % (half, b), [P, HALF], U8)
+            nc.vector.quantize_mx(out=z_codes[half, b][:].bitcast(FP8X4), scales=z_sc[half, b][:], in_=dst[:])
+
+        o_bank = {}
+
+        def out_pass(half, k, b):
+            if b == 0:
+                o_bank[half, k] = bank("o_bank_%d_%d" % (half, k), "b" if half == 0 else "a")
+            for u in range(2):
+                cols = slice((2 * k + u) * P, (2 * k + u + 1) * P)
+                nc.tensor.matmul_mx(
+                    out=o_bank[half, k][:, u * HALF : (u + 1) * HALF],
+                    lhsT=pg_codes[b][:, cols].bitcast(FP8X4),
+                    lhsT_scale=pg_sc[b][:, cols],
+                    rhs=z_codes[half, b][:].bitcast(FP8X4),
+                    rhs_scale=z_sc[half, b][:],
+                    start=(b == 0 and u == 0),
+                    stop=(b == RB - 1 and u == 1),
+                )
+
+        def finish(half, k, staged, on_vector):
+            for u in range(2):
+                c = 2 * k + u
+                src = o_bank[half, k][:, u * HALF : (u + 1) * HALF]
+                if on_vector:
+                    nc.vector.tensor_scalar(staged[:, c, :], src, slot_sb[:, c : c + 1], None, ALU.add)
+                else:
+                    nc.scalar.activation(staged[:, c, :], src, ACT.Identity, bias=slot_sb[:, c : c + 1], scale=1.0)
+            rows = out[2 * k * P : (2 * k + 2) * P, half * HALF : (half + 1) * HALF]
+            nc.sync.dma_start(out=rows.rearrange("(u p) j -> p u j", p=P), in_=staged[:, 2 * k : 2 * k + 2, :])
+
+        z00 = make_z(0, 0)
+        z01 = make_z(0, 1)
+        quant_page(1, page_woven)
+        quant_z(0, 0, z00, nc.scalar.copy)
+        quant_z(0, 1, z01, nc.vector.tensor_copy)
+        for b in range(RB):
+            for k in range(4):
+                out_pass(0, k, b)
+        z10 = make_z(1, 0)
+        z11 = make_z(1, 1)
+        quant_z(1, 0, z10, nc.scalar.copy)
+        quant_z(1, 1, z11, nc.vector.tensor_copy)
+        staged = [slab("staged_%d" % half, [P, T2 // P, HALF], F32) for half in range(2)]
+        for k in range(4):
+            finish(0, k, staged[0], False)
+        for b in range(RB):
+            for k in range(4):
+                out_pass(1, k, b)
+        for k in range(4):
+            finish(1, k, staged[1], k % 2 == 0)

@@ -40,7 +40,7 @@ def tile_list_canteen_menu_rotation_kernel(
             return ring.tile(shape, dtype, name=name, tag="slab", bufs=7, align_bytes=64)
 
         def bank(name, tag):
-            return psum.tile([P, 512], F32, name=name, tag=tag, bufs=4)
+            return psum.tile([P, 512], F32, name=name, tag=tag, bufs=4 if tag == "b" else 2)
 
         idx = held("idx", [P, S // 16], U16)
         idx2 = held("idx2", [P, S // 16], U16)
@@ -66,13 +66,13 @@ def tile_list_canteen_menu_rotation_kernel(
             nc.sync.dma_start(out=words[:], in_=tab_words[a].rearrange("p t i -> p (t i)").bitcast(I32))
             return words
 
-        resid_rows = resid.rearrange("(b p t) j -> b t p j", b=RB, t=PACK)
+        resid_rows = resid.rearrange("(b p t) j -> b p t j", b=RB, t=PACK)
         page_rows = page0.rearrange("(b p t) m -> b t p m", b=RB, t=PACK)
-        res = [held("res_%d" % i, [P, S], F32) for i in range(RB * PACK)]
+        res_first = held("res_first", [P, S], F32)
+        res_rest = held("res_rest", [P, PACK - 1, S], F32)
+        res_high = held("res_high", [P, PACK, S], F32)
+        res = [res_first[:]] + [res_rest[:, t, :] for t in range(PACK - 1)] + [res_high[:, t, :] for t in range(PACK)]
         page = [held("page_%d" % i, [P, T2], F32) for i in range(RB * PACK)]
-
-        def load_res(i):
-            nc.sync.dma_start(out=res[i][:], in_=resid_rows[i // PACK, i % PACK])
 
         def load_page(i):
             nc.sync.dma_start(out=page[i][:], in_=page_rows[i // PACK, i % PACK])
@@ -84,44 +84,41 @@ def tile_list_canteen_menu_rotation_kernel(
         tab.append(load_tab(0))
         nc.sync.dma_start(idx[:], offs)
         for q in range(4):
-            nc.scalar.dma_start(
+            nc.sync.dma_start(
                 out=tab_sc[32 * q : 32 * q + 4 * KA, :].bitcast(I32),
                 in_=tab_scales[:, 4 * q : 4 * q + 4, :].bitcast(I32),
             )
         w1_raw[0, 1] = load_w1(0, 1)
-        tab.append(load_tab(1))
-        w1_raw[0, 2] = load_w1(0, 2)
         for q in range(4):
-            nc.scalar.dma_start(
+            nc.sync.dma_start(
                 out=w4_sc_raw[32 * q : 32 * q + 4, :, :].bitcast(I32),
                 in_=w4_scales[:, 4 * q : 4 * q + 4, :].rearrange("a r n -> r a n").bitcast(I32),
             )
+        w1_raw[0, 2] = load_w1(0, 2)
+        tab.append(load_tab(1))
         wg_first = held("wg_first", [P, S], F32)
         wg_rest = held("wg_rest", [P, PACK - 1, S], F32)
         wg_rows = wgs.rearrange("(q t) j -> q t j", t=PACK)
         tab.append(load_tab(2))
-        load_res(0)
+        nc.sync.dma_start(out=res_first[:], in_=resid_rows[0, :, 0, :])
         for q in range(4):
             nc.sync.dma_start(out=wg_first[32 * q : 32 * q + 32, :], in_=wg_rows[:, 0, :])
         nc.sync.dma_start(idx2[:], offs2)
         load_page(0)
-        load_res(1)
+        nc.sync.dma_start(out=res_rest[:], in_=resid_rows[0, :, 1:PACK, :])
         nc.sync.dma_start(idx3[:], offs3)
         for q in range(4):
             nc.sync.dma_start(out=wg_rest[32 * q : 32 * q + 32, :, :], in_=wg_rows[:, 1:PACK, :])
         load_page(1)
-        load_res(2)
         w1_raw[1, 0] = load_w1(1, 0)
-        w1_raw[1, 1] = load_w1(1, 1)
         load_page(2)
-        load_res(3)
+        w1_raw[1, 1] = load_w1(1, 1)
         w1_raw[1, 2] = load_w1(1, 2)
         load_page(3)
-        for i in range(PACK, RB * PACK):
-            load_res(i)
+        load_page(PACK)
+        nc.sync.dma_start(out=res_high[:], in_=resid_rows[1])
         for i in range(PACK + 1, RB * PACK):
             load_page(i)
-        load_page(PACK)
         least_sb = held("least_sb", [P, RB, PACK], F32)
         gain_sb = held("gain_sb", [P, RB, PACK], F32)
         slot_sb = held("slot_sb", [P, T2 // P], F32)
@@ -174,10 +171,14 @@ def tile_list_canteen_menu_rotation_kernel(
         nc.vector.tensor_copy(v_sc[:], tab_sc[:].indirect(idx[:]))
         gather_tab(0)
         quant_w1(0, 0, 0)
-        gather_tab(1)
         quant_w1(0, 1, 0)
-        quant_w1(0, 2, 48)
-        gather_tab(2)
+        gather_tab(1)
+        quant_w1(0, 2, 0)
+        for half in range(2):
+            cols = slice(half * HALF, (half + 1) * HALF)
+            nc.vector.tensor_copy(
+                v[KA - 1][:, cols], tab[KA - 1][:].bitcast(U32).indirect(idx[:, half * 16 : (half + 1) * 16])
+            )
 
         h_bank = {}
 
@@ -196,29 +197,50 @@ def tile_list_canteen_menu_rotation_kernel(
                 stop=(a == KA - 1),
             )
 
+        h_first = [bank("h_first_%d" % half, "a") for half in range(2)]
         for a in range(KA):
-            for i in range(PACK):
+            for half in range(2):
+                cols = slice(half * HALF, (half + 1) * HALF)
+                nc.tensor.matmul_mx(
+                    out=h_first[half][:, 0:HALF],
+                    lhsT=w1_codes[0, a][:, 0:P].bitcast(FP8X4),
+                    lhsT_scale=w1_sc[0, a][:, 0:P],
+                    rhs=v[a][:, cols].bitcast(FP8X4),
+                    rhs_scale=v_sc[4 * a : P, cols],
+                    start=(a == 0),
+                    stop=(a == KA - 1),
+                )
+            for i in range(1, PACK):
                 h_pass(i, a)
 
         x_planes = [held("x_planes_%d" % b, [P, PACK, NP], BF16) for b in range(RB)]
-        x_codes = [held("x_codes_%d" % b, [P, NP], U32) for b in range(RB)]
+        x_codes = {1: held("x_codes_1", [P, NP], U32)}
         x_sc = [held("x_sc_%d" % b, [P, NP], U8) for b in range(RB)]
         pg_codes = [held("pg_codes_%d" % b, [P, T2], U32) for b in range(RB)]
-        pg_sc = [held("pg_sc_%d" % b, [P, T2], U8) for b in range(RB)]
+        pg_sc = {1: held("pg_sc_1", [P, T2], U8)}
 
         def woven(name):
             return ring.tile([P, PACK * HALF], BF16, name=name, tag="woven", bufs=4, align_bytes=64)
 
         def weave(copy, dst, planes):
             copy(
-                out=dst[:].rearrange("p (c i t) -> p c t i", i=4, t=PACK),
+                out=dst.rearrange("p (c i t) -> p c t i", i=4, t=PACK),
                 in_=planes.rearrange("p t (c i) -> p c t i", i=4),
             )
 
-        def quant_x(b, half, copy):
+        x_woven = {}
+
+        def weave_x(b, half, copy):
+            if (b, half) == (1, 0):
+                dst = ring.tile([P, PACK * HALF], BF16, name="x_woven_1_0", tag="x_first", bufs=1, align_bytes=64)
+            else:
+                dst = woven("x_woven_%d_%d" % (b, half))
+            weave(copy, dst[:], x_planes[b][:, :, half * HALF : (half + 1) * HALF])
+            x_woven[b, half] = dst
+
+        def quant_x(b, half):
             cols = slice(half * HALF, (half + 1) * HALF)
-            dst = woven("x_woven_%d_%d" % (b, half))
-            weave(copy, dst, x_planes[b][:, :, cols])
+            dst = x_woven[b, half]
             nc.vector.quantize_mx(out=x_codes[b][:, cols].bitcast(FP8X4), scales=x_sc[b][:, cols], in_=dst[:])
 
         def weave_page(b):
@@ -228,17 +250,18 @@ def tile_list_canteen_menu_rotation_kernel(
             return whole
 
         def quant_page(b, whole):
-            nc.vector.quantize_mx(
-                out=pg_codes[b][:].bitcast(FP8X4),
-                scales=pg_sc[b][:],
-                in_=whole[:].rearrange("p m u -> p (m u)").bitcast(BF16),
-            )
+            for cols in (slice(0, T2 // 2), slice(T2 // 2, T2)):
+                nc.vector.quantize_mx(
+                    out=pg_codes[b][:, cols].bitcast(FP8X4),
+                    scales=pg_sc[b][:, cols],
+                    in_=whole[:, cols, :].rearrange("p m u -> p (m u)").bitcast(BF16),
+                )
 
         y_bank = {}
 
         def y_pass(half, k, a):
             if a == 0:
-                y_bank[half, k] = bank("y_bank_%d_%d" % (half, k), "b" if half == 0 else "a")
+                y_bank[half, k] = bank("y_bank_%d_%d" % (half, k), "b" if half == 0 else ("c" if k < 2 else "a"))
             for u in range(2):
                 n = 2 * k + u
                 for c in range(2):
@@ -259,14 +282,23 @@ def tile_list_canteen_menu_rotation_kernel(
         def add_resid(i):
             if i == PACK - 1:
                 h[i] = ring.tile([P, S], F32, name="h_%d" % i, tag="last_bf", bufs=1, align_bytes=64)
+            elif i == RB * PACK - 1:
+                h[i] = ring.tile([P, S], F32, name="h_%d" % i, tag="last_raw", bufs=1, align_bytes=64)
             else:
                 h[i] = ring.tile([P, S], F32, name="h_%d" % i, tag="h", bufs=2)
-            nc.vector.tensor_tensor(h[i][:], h_bank[i][:], res[i][:], ALU.add)
+            nc.vector.tensor_tensor(h[i][:], h_bank[i][:], res[i], ALU.add)
 
-        add_resid(0)
+        for half in range(2):
+            cols = slice(half * HALF, (half + 1) * HALF)
+            part = ring.tile([P, HALF], F32, name="h_first_%d" % half, tag="h", bufs=2)
+            nc.vector.tensor_tensor(part[:], h_first[half][:, 0:HALF], res_first[:, cols], ALU.add)
+            nc.vector.tensor_tensor(
+                page[0][:].indirect(idx2[:, half * 16 : (half + 1) * 16]), part[:], wg_first[:, cols], ALU.mult
+            )
         for i in range(RB * PACK):
             b, t = divmod(i, PACK)
-            nc.vector.tensor_tensor(page[i][:].indirect(idx2[:]), h[i][:], wg(t), ALU.mult)
+            if i > 0:
+                nc.vector.tensor_tensor(page[i][:].indirect(idx2[:]), h[i][:], wg(t), ALU.mult)
             if i < KA:
                 quant_w1(1, i, 0)
             if i == KA - 1:
@@ -275,9 +307,12 @@ def tile_list_canteen_menu_rotation_kernel(
                         h_pass(i2, a)
             if i + 1 < RB * PACK:
                 add_resid(i + 1)
-            nc.vector.tensor_copy(x_planes[b][:, t, :], page[i][:].indirect(idx3[:]))
             if i == RB * PACK - 1:
-                quant_x(b, 0, nc.vector.tensor_copy)
+                x_codes[0] = ring.tile([P, NP], U32, name="x_codes_0", tag="last_raw", bufs=1, align_bytes=64)
+                quant_x(0, 0)
+                for k in range(4):
+                    y_pass(0, k, 0)
+            nc.vector.tensor_copy(x_planes[b][:, t, :], page[i][:].indirect(idx3[:]))
             if i == PACK:
                 pairs.append(slab("pairs_1", [P, 2, T2, 2], BF16))
             if i == KA - 1:
@@ -286,20 +321,23 @@ def tile_list_canteen_menu_rotation_kernel(
                     nc.scalar.copy(out=pairs[0][:, i2 // 2, :, i2 % 2], in_=page[i2][:])
             if i >= KA - 1:
                 nc.scalar.copy(out=pairs[b][:, t // 2, :, t % 2], in_=page[i][:])
-            if i == PACK - 1:
-                quant_x(0, 0, nc.scalar.copy)
-                quant_x(0, 1, nc.scalar.copy)
-                quant_page(0, weave_page(0))
-                for k in range(4):
-                    y_pass(0, k, 0)
-        page_woven = weave_page(1)
+            if i == PACK:
+                weave_x(0, 0, nc.scalar.copy)
+                weave_x(0, 1, nc.scalar.copy)
+                page_woven = [weave_page(0)]
+        weave_x(1, 0, nc.vector.tensor_copy)
+        quant_x(0, 1)
+        quant_x(1, 0)
         for k in range(4):
             y_pass(0, k, 1)
-        quant_x(1, 1, nc.scalar.copy)
-        for k in range(4):
-            y_pass(1, k, 0)
-        for k in range(4):
-            y_pass(1, k, 1)
+        weave_x(1, 1, nc.scalar.copy)
+        page_woven.append(weave_page(1))
+        pg_sc[0] = ring.tile([P, T2], U8, name="pg_sc_0", tag="x_first", bufs=1, align_bytes=64)
+        quant_page(0, page_woven[0])
+        quant_x(1, 1)
+        for a in range(RB):
+            for k in range(4):
+                y_pass(1, k, a)
 
         z_codes = {}
         z_sc = {}
@@ -319,57 +357,72 @@ def tile_list_canteen_menu_rotation_kernel(
             return planes
 
         def quant_z(half, b, planes, copy):
-            dst = woven("z_woven_%d_%d" % (half, b))
-            weave(copy, dst, planes[:])
+            if half == 1:
+                dst = ring.tile([P, PACK * HALF], BF16, name="z_woven_1_%d" % b, tag="z_last", bufs=1, align_bytes=64)
+            else:
+                dst = woven("z_woven_%d_%d" % (half, b))
+            if copy is None:
+                cut = 96
+                weave(nc.scalar.copy, dst[:, 0 : PACK * cut], planes[:, :, 0:cut])
+                weave(nc.vector.tensor_copy, dst[:, PACK * cut : PACK * HALF], planes[:, :, cut:HALF])
+            else:
+                weave(copy, dst[:], planes[:])
             z_codes[half, b] = held("z_codes_%d_%d" % (half, b), [P, HALF], U32)
             z_sc[half, b] = held("z_sc_%d_%d" % (half, b), [P, HALF], U8)
             nc.vector.quantize_mx(out=z_codes[half, b][:].bitcast(FP8X4), scales=z_sc[half, b][:], in_=dst[:])
 
         o_bank = {}
 
-        def out_pass(half, k, b):
-            if b == 0:
-                o_bank[half, k] = bank("o_bank_%d_%d" % (half, k), "b" if half == 0 else "a")
-            for u in range(2):
-                cols = slice((2 * k + u) * P, (2 * k + u + 1) * P)
-                nc.tensor.matmul_mx(
-                    out=o_bank[half, k][:, u * HALF : (u + 1) * HALF],
-                    lhsT=pg_codes[b][:, cols].bitcast(FP8X4),
-                    lhsT_scale=pg_sc[b][:, cols],
-                    rhs=z_codes[half, b][:].bitcast(FP8X4),
-                    rhs_scale=z_sc[half, b][:],
-                    start=(b == 0 and u == 0),
-                    stop=(b == RB - 1 and u == 1),
-                )
+        def out_pass(half, c, b):
+            k, u = divmod(c, 2)
+            if half == 0:
+                if b == 0 and u == 0:
+                    o_bank[0, c] = bank("o_bank_0_%d" % k, "b")
+                    o_bank[0, c + 1] = o_bank[0, c]
+                dst = o_bank[0, c][:, u * HALF : (u + 1) * HALF]
+                first, last = (b == 0 and u == 0), (b == RB - 1 and u == 1)
+            else:
+                if b == 0:
+                    o_bank[1, c] = bank("o_bank_1_%d" % c, ("c", "c", "a", "a", "b", "b", "b", "b")[c])
+                dst = o_bank[1, c][:, 0:HALF]
+                first, last = b == 0, b == RB - 1
+            cols = slice(c * P, (c + 1) * P)
+            nc.tensor.matmul_mx(
+                out=dst,
+                lhsT=pg_codes[b][:, cols].bitcast(FP8X4),
+                lhsT_scale=pg_sc[b][:, cols],
+                rhs=z_codes[half, b][:].bitcast(FP8X4),
+                rhs_scale=z_sc[half, b][:],
+                start=first,
+                stop=last,
+            )
+            return dst
 
-        def finish(half, k, staged, on_vector):
-            for u in range(2):
-                c = 2 * k + u
-                src = o_bank[half, k][:, u * HALF : (u + 1) * HALF]
-                if on_vector:
-                    nc.vector.tensor_scalar(staged[:, c, :], src, slot_sb[:, c : c + 1], None, ALU.add)
+        def finish(half, k, srcs, staged):
+            for c in (2 * k, 2 * k + 1):
+                if half == 1 and c % 2 == 0:
+                    nc.vector.tensor_scalar(staged[:, c, :], srcs[c], slot_sb[:, c : c + 1], None, ALU.add)
                 else:
-                    nc.scalar.activation(staged[:, c, :], src, ACT.Identity, bias=slot_sb[:, c : c + 1], scale=1.0)
+                    nc.scalar.activation(staged[:, c, :], srcs[c], ACT.Identity, bias=slot_sb[:, c : c + 1], scale=1.0)
             rows = out[2 * k * P : (2 * k + 2) * P, half * HALF : (half + 1) * HALF]
             nc.sync.dma_start(out=rows.rearrange("(u p) j -> p u j", p=P), in_=staged[:, 2 * k : 2 * k + 2, :])
 
         z00 = make_z(0, 0)
         z01 = make_z(0, 1)
-        quant_page(1, page_woven)
         quant_z(0, 0, z00, nc.scalar.copy)
-        quant_z(0, 1, z01, nc.vector.tensor_copy)
+        quant_z(0, 1, z01, nc.scalar.copy)
+        quant_page(1, page_woven[1])
         for b in range(RB):
-            for k in range(4):
-                out_pass(0, k, b)
-        z10 = make_z(1, 0)
-        z11 = make_z(1, 1)
-        quant_z(1, 0, z10, nc.scalar.copy)
-        quant_z(1, 1, z11, nc.vector.tensor_copy)
+            srcs = [out_pass(0, c, b) for c in range(T2 // P)]
         staged = [slab("staged_%d" % half, [P, T2 // P, HALF], F32) for half in range(2)]
+        z10 = make_z(1, 0)
+        quant_z(1, 0, z10, nc.scalar.copy)
         for k in range(4):
-            finish(0, k, staged[0], False)
-        for b in range(RB):
-            for k in range(4):
-                out_pass(1, k, b)
+            finish(0, k, srcs, staged[0])
+        z11 = make_z(1, 1)
+        for c in range(T2 // P):
+            out_pass(1, c, 0)
+        quant_z(1, 1, z11, nc.vector.tensor_copy)
+        srcs = [out_pass(1, c, 1) for c in range(T2 // P)]
         for k in range(4):
-            finish(1, k, staged[1], k % 2 == 0)
+            finish(1, k, srcs, staged[1])

@@ -48,9 +48,9 @@ def tile_list_canteen_menu_rotation_kernel(
 
         tab_sc = held("tab_sc", [P, T], U8)
         w4_raw = held("w4_raw", [P, RB, 2 * H], U8)
-        w4_sc_raw = held("w4_sc_raw", [P, RB, H], U8)
-        nc.gpsimd.memset(tab_sc[:].bitcast(I32), 0)
-        nc.gpsimd.memset(w4_sc_raw[:].rearrange("p a n -> p (a n)").bitcast(I32), 0)
+        w4_sc_raw = ring.tile([P, RB, H], U8, name="w4_sc_raw", tag="early_sc", bufs=1, align_bytes=64)
+        nc.vector.memset(tab_sc[:].bitcast(I32), 0)
+        nc.vector.memset(w4_sc_raw[:].rearrange("p a n -> p (a n)").bitcast(I32), 0)
 
         def load_w1(b, a):
             if (b, a) == (RB - 1, KA - 1):
@@ -68,10 +68,11 @@ def tile_list_canteen_menu_rotation_kernel(
 
         resid_rows = resid.rearrange("(b p t) j -> b p t j", b=RB, t=PACK)
         page_rows = page0.rearrange("(b p t) m -> b t p m", b=RB, t=PACK)
-        res_first = held("res_first", [P, S], F32)
-        res_rest = held("res_rest", [P, PACK - 1, S], F32)
-        res_high = held("res_high", [P, PACK, S], F32)
-        res = [res_first[:]] + [res_rest[:, t, :] for t in range(PACK - 1)] + [res_high[:, t, :] for t in range(PACK)]
+        res = [held("res_%d" % i, [P, S], F32) for i in range(RB * PACK)]
+
+        def load_res(i):
+            nc.sync.dma_start(out=res[i][:], in_=resid_rows[i // PACK, :, i % PACK, :])
+
         page = [held("page_%d" % i, [P, T2], F32) for i in range(RB * PACK)]
 
         def load_page(i):
@@ -84,41 +85,44 @@ def tile_list_canteen_menu_rotation_kernel(
         tab.append(load_tab(0))
         nc.sync.dma_start(idx[:], offs)
         for q in range(4):
-            nc.sync.dma_start(
+            nc.gpsimd.dma_start(
                 out=tab_sc[32 * q : 32 * q + 4 * KA, :].bitcast(I32),
                 in_=tab_scales[:, 4 * q : 4 * q + 4, :].bitcast(I32),
             )
-        w1_raw[0, 1] = load_w1(0, 1)
         for q in range(4):
             nc.sync.dma_start(
                 out=w4_sc_raw[32 * q : 32 * q + 4, :, :].bitcast(I32),
                 in_=w4_scales[:, 4 * q : 4 * q + 4, :].rearrange("a r n -> r a n").bitcast(I32),
             )
+        w1_raw[0, 1] = load_w1(0, 1)
         w1_raw[0, 2] = load_w1(0, 2)
         tab.append(load_tab(1))
         wg_first = held("wg_first", [P, S], F32)
-        wg_rest = held("wg_rest", [P, PACK - 1, S], F32)
+        wg_mid = held("wg_mid", [P, 2, S], F32)
+        wg_last = held("wg_last", [P, S], F32)
         wg_rows = wgs.rearrange("(q t) j -> q t j", t=PACK)
         tab.append(load_tab(2))
-        nc.sync.dma_start(out=res_first[:], in_=resid_rows[0, :, 0, :])
+        load_res(0)
         for q in range(4):
             nc.sync.dma_start(out=wg_first[32 * q : 32 * q + 32, :], in_=wg_rows[:, 0, :])
         nc.sync.dma_start(idx2[:], offs2)
         load_page(0)
-        nc.sync.dma_start(out=res_rest[:], in_=resid_rows[0, :, 1:PACK, :])
+        load_res(1)
         nc.sync.dma_start(idx3[:], offs3)
         for q in range(4):
-            nc.sync.dma_start(out=wg_rest[32 * q : 32 * q + 32, :, :], in_=wg_rows[:, 1:PACK, :])
+            nc.sync.dma_start(out=wg_mid[32 * q : 32 * q + 32, :, :], in_=wg_rows[:, 1:3, :])
         load_page(1)
+        load_res(2)
         w1_raw[1, 0] = load_w1(1, 0)
         load_page(2)
+        load_res(3)
         w1_raw[1, 1] = load_w1(1, 1)
         w1_raw[1, 2] = load_w1(1, 2)
-        load_page(3)
-        load_page(PACK)
-        nc.sync.dma_start(out=res_high[:], in_=resid_rows[1])
-        for i in range(PACK + 1, RB * PACK):
+        for q in range(4):
+            nc.sync.dma_start(out=wg_last[32 * q : 32 * q + 32, :], in_=wg_rows[:, 3, :])
+        for i in range(PACK - 1, RB * PACK - 1):
             load_page(i)
+            load_res(i + 1)
         least_sb = held("least_sb", [P, RB, PACK], F32)
         gain_sb = held("gain_sb", [P, RB, PACK], F32)
         slot_sb = held("slot_sb", [P, T2 // P], F32)
@@ -126,23 +130,24 @@ def tile_list_canteen_menu_rotation_kernel(
         nc.sync.dma_start(out=gain_sb[:], in_=gain.rearrange("(b p t) -> p b t", b=RB, t=PACK))
         with nc.allow_non_contiguous_dma(reason="one value of slot to a partition"):
             nc.sync.dma_start(out=slot_sb[:], in_=slot.rearrange("(c p) -> p c", p=P))
+        load_page(RB * PACK - 1)
 
         def wg(t):
-            return wg_first[:] if t == 0 else wg_rest[:, t - 1, :]
+            return (wg_first[:], wg_mid[:, 0, :], wg_mid[:, 1, :], wg_last[:])[t]
 
         w4 = held("w4", [P, RB, 2 * H], U8)
         w4_sc = held("w4_sc", [P, RB, H], U8)
         for a in range(RB):
             nc.vector.tensor_copy(
-                out=w4[:, a, :].rearrange("p (b t m e) -> p b t m e", b=RB, t=PACK, e=2),
-                in_=w4_raw[:, a, :].rearrange("p (b m t e) -> p b t m e", b=RB, t=PACK, e=2),
+                out=w4[:, a, :].bitcast(U16).rearrange("p (b t m) -> p b t m", b=RB, t=PACK),
+                in_=w4_raw[:, a, :].bitcast(U16).rearrange("p (b m t) -> p b t m", b=RB, t=PACK),
             )
         nc.vector.tensor_copy(
             out=w4_sc[:].rearrange("p a (b t m) -> p (a b) t m", b=RB, t=PACK),
             in_=w4_sc_raw[:].rearrange("p a (b m t) -> p (a b) t m", b=RB, t=PACK),
         )
 
-        v_sc = held("v_sc", [P, S], U8)
+        v_sc = ring.tile([P, S], U8, name="v_sc", tag="early_sc", bufs=1, align_bytes=64)
         v = [held("v_%d" % a, [P, S], U32) for a in range(KA)]
         w1_codes = {}
         w1_sc = {}
@@ -151,14 +156,9 @@ def tile_list_canteen_menu_rotation_kernel(
             nc.vector.tensor_copy(v[a][:], tab[a][:].bitcast(U32).indirect(idx[:]))
 
         def quant_w1(b, a, split):
-            if (b, a) == (RB - 1, KA - 1):
-                staged = ring.tile([P, PACK * KP], BF16, name="w1_bf_last", tag="last_bf", bufs=1, align_bytes=64)
-            else:
-                staged = ring.tile(
-                    [P, PACK * KP], BF16, name="w1_bf_%d_%d" % (b, a), tag="w1_bf", bufs=2, align_bytes=64
-                )
-            dst = staged[:].rearrange("p (t m i) -> p m i t", t=PACK, i=PACK)
-            src = w1_raw[b, a][:].rearrange("p i (m t) -> p m i t", t=PACK)
+            staged = ring.tile([P, PACK * KP], BF16, name="w1_bf_%d_%d" % (b, a), tag="w1_bf", bufs=3, align_bytes=64)
+            dst = staged[:].rearrange("p (t m i) -> p m t i", t=PACK, i=PACK)
+            src = w1_raw[b, a][:].rearrange("p i (m t) -> p m t i", t=PACK)
             if split:
                 nc.scalar.copy(out=dst[:, 0:split], in_=src[:, 0:split])
                 nc.vector.tensor_copy(out=dst[:, split:P], in_=src[:, split:P])
@@ -173,7 +173,7 @@ def tile_list_canteen_menu_rotation_kernel(
         quant_w1(0, 0, 0)
         quant_w1(0, 1, 0)
         gather_tab(1)
-        quant_w1(0, 2, 0)
+        quant_w1(0, 2, 96)
         for half in range(2):
             cols = slice(half * HALF, (half + 1) * HALF)
             nc.vector.tensor_copy(
@@ -280,18 +280,16 @@ def tile_list_canteen_menu_rotation_kernel(
         pairs = []
 
         def add_resid(i):
-            if i == PACK - 1:
-                h[i] = ring.tile([P, S], F32, name="h_%d" % i, tag="last_bf", bufs=1, align_bytes=64)
-            elif i == RB * PACK - 1:
-                h[i] = ring.tile([P, S], F32, name="h_%d" % i, tag="last_raw", bufs=1, align_bytes=64)
+            if i == RB * PACK - 1:
+                h[i] = ring.tile([P, S], F32, name="h_%d" % i, tag="h_last", bufs=1, align_bytes=64)
             else:
                 h[i] = ring.tile([P, S], F32, name="h_%d" % i, tag="h", bufs=2)
-            nc.vector.tensor_tensor(h[i][:], h_bank[i][:], res[i], ALU.add)
+            nc.vector.tensor_tensor(h[i][:], h_bank[i][:], res[i][:], ALU.add)
 
         for half in range(2):
             cols = slice(half * HALF, (half + 1) * HALF)
             part = ring.tile([P, HALF], F32, name="h_first_%d" % half, tag="h", bufs=2)
-            nc.vector.tensor_tensor(part[:], h_first[half][:, 0:HALF], res_first[:, cols], ALU.add)
+            nc.vector.tensor_tensor(part[:], h_first[half][:, 0:HALF], res[0][:, cols], ALU.add)
             nc.vector.tensor_tensor(
                 page[0][:].indirect(idx2[:, half * 16 : (half + 1) * 16]), part[:], wg_first[:, cols], ALU.mult
             )
@@ -308,7 +306,7 @@ def tile_list_canteen_menu_rotation_kernel(
             if i + 1 < RB * PACK:
                 add_resid(i + 1)
             if i == RB * PACK - 1:
-                x_codes[0] = ring.tile([P, NP], U32, name="x_codes_0", tag="last_raw", bufs=1, align_bytes=64)
+                x_codes[0] = ring.tile([P, NP], U32, name="x_codes_0", tag="h_last", bufs=1, align_bytes=64)
                 quant_x(0, 0)
                 for k in range(4):
                     y_pass(0, k, 0)

@@ -213,7 +213,7 @@ def tile_list_canteen_menu_rotation_kernel(
             for i in range(1, PACK):
                 h_pass(i, a)
 
-        x_planes = [held("x_planes_%d" % b, [P, PACK, NP], BF16) for b in range(RB)]
+        x_planes = [held("x_planes_%d" % b, [P, PACK, NP], F32) for b in range(RB)]
         x_codes = {1: held("x_codes_1", [P, NP], U32)}
         x_sc = [held("x_sc_%d" % b, [P, NP], U8) for b in range(RB)]
         pg_codes = [held("pg_codes_%d" % b, [P, T2], U32) for b in range(RB)]
@@ -355,12 +355,9 @@ def tile_list_canteen_menu_rotation_kernel(
             return planes
 
         def quant_z(half, b, planes, copy):
-            if half == 1:
-                dst = ring.tile([P, PACK * HALF], BF16, name="z_woven_1_%d" % b, tag="z_last", bufs=1, align_bytes=64)
-            else:
-                dst = woven("z_woven_%d_%d" % (half, b))
+            dst = woven("z_woven_%d_%d" % (half, b))
             if copy is None:
-                cut = 96
+                cut = 192
                 weave(nc.scalar.copy, dst[:, 0 : PACK * cut], planes[:, :, 0:cut])
                 weave(nc.vector.tensor_copy, dst[:, PACK * cut : PACK * HALF], planes[:, :, cut:HALF])
             else:
@@ -402,8 +399,11 @@ def tile_list_canteen_menu_rotation_kernel(
                     nc.vector.tensor_scalar(staged[:, c, :], srcs[c], slot_sb[:, c : c + 1], None, ALU.add)
                 else:
                     nc.scalar.activation(staged[:, c, :], srcs[c], ACT.Identity, bias=slot_sb[:, c : c + 1], scale=1.0)
-            rows = out[2 * k * P : (2 * k + 2) * P, half * HALF : (half + 1) * HALF]
-            nc.sync.dma_start(out=rows.rearrange("(u p) j -> p u j", p=P), in_=staged[:, 2 * k : 2 * k + 2, :])
+                if half == 1:
+                    nc.sync.dma_start(out=out[c * P : (c + 1) * P, HALF:NP], in_=staged[:, c, :])
+            if half == 0:
+                rows = out[2 * k * P : (2 * k + 2) * P, 0:HALF]
+                nc.sync.dma_start(out=rows.rearrange("(u p) j -> p u j", p=P), in_=staged[:, 2 * k : 2 * k + 2, :])
 
         z00 = make_z(0, 0)
         z01 = make_z(0, 1)
@@ -414,7 +414,7 @@ def tile_list_canteen_menu_rotation_kernel(
             srcs = [out_pass(0, c, b) for c in range(T2 // P)]
         staged = [slab("staged_%d" % half, [P, T2 // P, HALF], F32) for half in range(2)]
         z10 = make_z(1, 0)
-        quant_z(1, 0, z10, nc.scalar.copy)
+        quant_z(1, 0, z10, None)
         for k in range(4):
             finish(0, k, srcs, staged[0])
         z11 = make_z(1, 1)

@@ -73,7 +73,7 @@ def tile_list_canteen_menu_rotation_kernel(
         def load_res(i):
             nc.sync.dma_start(out=res[i][:], in_=resid_rows[i // PACK, :, i % PACK, :])
 
-        page = [held("page_%d" % i, [P, T2], F32) for i in range(RB * PACK)]
+        page = [held("page_%d" % i, [P, T2], F32) for i in range(RB * PACK - 1)]
 
         def load_page(i):
             nc.sync.dma_start(out=page[i][:], in_=page_rows[i // PACK, i % PACK])
@@ -117,10 +117,12 @@ def tile_list_canteen_menu_rotation_kernel(
         load_page(2)
         load_res(3)
         w1_raw[1, 1] = load_w1(1, 1)
-        w1_raw[1, 2] = load_w1(1, 2)
         for q in range(4):
             nc.sync.dma_start(out=wg_last[32 * q : 32 * q + 32, :], in_=wg_rows[:, 3, :])
-        for i in range(PACK - 1, RB * PACK - 1):
+        w1_raw[1, 2] = load_w1(1, 2)
+        load_res(PACK)
+        load_page(PACK - 1)
+        for i in range(PACK, RB * PACK - 1):
             load_page(i)
             load_res(i + 1)
         least_sb = held("least_sb", [P, RB, PACK], F32)
@@ -130,7 +132,6 @@ def tile_list_canteen_menu_rotation_kernel(
         nc.sync.dma_start(out=gain_sb[:], in_=gain.rearrange("(b p t) -> p b t", b=RB, t=PACK))
         with nc.allow_non_contiguous_dma(reason="one value of slot to a partition"):
             nc.sync.dma_start(out=slot_sb[:], in_=slot.rearrange("(c p) -> p c", p=P))
-        load_page(RB * PACK - 1)
 
         def wg(t):
             return (wg_first[:], wg_mid[:, 0, :], wg_mid[:, 1, :], wg_last[:])[t]
@@ -235,7 +236,12 @@ def tile_list_canteen_menu_rotation_kernel(
                 dst = ring.tile([P, PACK * HALF], BF16, name="x_woven_1_0", tag="x_first", bufs=1, align_bytes=64)
             else:
                 dst = woven("x_woven_%d_%d" % (b, half))
-            weave(copy, dst[:], x_planes[b][:, :, half * HALF : (half + 1) * HALF])
+            planes = x_planes[b][:, :, half * HALF : (half + 1) * HALF]
+            if copy is None:
+                weave(nc.scalar.copy, dst[:, 0 : PACK * 64], planes[:, :, 0:64])
+                weave(nc.vector.tensor_copy, dst[:, PACK * 64 : PACK * HALF], planes[:, :, 64:HALF])
+            else:
+                weave(copy, dst[:], planes)
             x_woven[b, half] = dst
 
         def quant_x(b, half):
@@ -243,19 +249,24 @@ def tile_list_canteen_menu_rotation_kernel(
             dst = x_woven[b, half]
             nc.vector.quantize_mx(out=x_codes[b][:, cols].bitcast(FP8X4), scales=x_sc[b][:, cols], in_=dst[:])
 
-        def weave_page(b):
-            whole = slab("pg_woven_%d" % b, [P, T2, 2], F32)
-            words = pairs[b][:].rearrange("p u m e -> p u (m e)").bitcast(F32)
-            nc.scalar.copy(out=whole[:], in_=words.rearrange("p u m -> p m u"))
-            return whole
+        page_woven = {}
+        PART = T2 // 4
 
-        def quant_page(b, whole):
-            for cols in (slice(0, T2 // 2), slice(T2 // 2, T2)):
-                nc.vector.quantize_mx(
-                    out=pg_codes[b][:, cols].bitcast(FP8X4),
-                    scales=pg_sc[b][:, cols],
-                    in_=whole[:, cols, :].rearrange("p m u -> p (m u)").bitcast(BF16),
-                )
+        def weave_page(b, part):
+            if part == 0:
+                page_woven[b] = slab("pg_woven_%d" % b, [P, PACK * T2], BF16)
+            weave(
+                nc.scalar.copy,
+                page_woven[b][:, PACK * PART * part : PACK * PART * (part + 1)],
+                page_planes[b][:, :, PART * part : PART * (part + 1)],
+            )
+
+        def quant_page(b, lo, hi):
+            nc.vector.quantize_mx(
+                out=pg_codes[b][:, PART * lo : PART * hi].bitcast(FP8X4),
+                scales=pg_sc[b][:, PART * lo : PART * hi],
+                in_=page_woven[b][:, PACK * PART * lo : PACK * PART * hi],
+            )
 
         y_bank = {}
 
@@ -277,7 +288,7 @@ def tile_list_canteen_menu_rotation_kernel(
                     )
 
         h = {}
-        pairs = []
+        page_planes = []
 
         def add_resid(i):
             if i == RB * PACK - 1:
@@ -312,26 +323,31 @@ def tile_list_canteen_menu_rotation_kernel(
                     y_pass(0, k, 0)
             nc.vector.tensor_copy(x_planes[b][:, t, :], page[i][:].indirect(idx3[:]))
             if i == PACK:
-                pairs.append(slab("pairs_1", [P, 2, T2, 2], BF16))
+                page_planes.append(slab("planes_1", [P, PACK, T2], BF16))
             if i == KA - 1:
-                pairs.append(ring.tile([P, 2, T2, 2], BF16, name="pairs_0", tag="last_raw", bufs=1, align_bytes=64))
+                page_planes.append(ring.tile([P, PACK, T2], BF16, name="planes_0", tag="last_raw", bufs=1, align_bytes=64))
                 for i2 in range(i):
-                    nc.scalar.copy(out=pairs[0][:, i2 // 2, :, i2 % 2], in_=page[i2][:])
+                    nc.scalar.copy(out=page_planes[0][:, i2, :], in_=page[i2][:])
             if i >= KA - 1:
-                nc.scalar.copy(out=pairs[b][:, t // 2, :, t % 2], in_=page[i][:])
-            if i == PACK:
+                nc.scalar.copy(out=page_planes[b][:, t, :], in_=page[i][:])
+            if i == PACK - 1:
                 weave_x(0, 0, nc.scalar.copy)
                 weave_x(0, 1, nc.scalar.copy)
-                page_woven = [weave_page(0)]
-        weave_x(1, 0, nc.vector.tensor_copy)
+                for part in range(4):
+                    weave_page(0, part)
+                page.append(ring.tile([P, T2], F32, name="page_last", tag="last_raw", bufs=1, align_bytes=64))
+                load_page(RB * PACK - 1)
+        weave_x(1, 0, None)
         quant_x(0, 1)
         quant_x(1, 0)
         for k in range(4):
             y_pass(0, k, 1)
         weave_x(1, 1, nc.scalar.copy)
-        page_woven.append(weave_page(1))
+        for part in range(3):
+            weave_page(1, part)
         pg_sc[0] = ring.tile([P, T2], U8, name="pg_sc_0", tag="x_first", bufs=1, align_bytes=64)
-        quant_page(0, page_woven[0])
+        quant_page(0, 0, 2)
+        quant_page(0, 2, 4)
         quant_x(1, 1)
         for a in range(RB):
             for k in range(4):
@@ -370,11 +386,11 @@ def tile_list_canteen_menu_rotation_kernel(
 
         def out_pass(half, c, b):
             k, u = divmod(c, 2)
-            if half == 0:
+            if half == 0 or k == 3:
                 if b == 0 and u == 0:
-                    o_bank[0, c] = bank("o_bank_0_%d" % k, "b")
-                    o_bank[0, c + 1] = o_bank[0, c]
-                dst = o_bank[0, c][:, u * HALF : (u + 1) * HALF]
+                    o_bank[half, c] = bank("o_bank_%d_%d" % (half, c), "b")
+                    o_bank[half, c + 1] = o_bank[half, c]
+                dst = o_bank[half, c][:, u * HALF : (u + 1) * HALF]
                 first, last = (b == 0 and u == 0), (b == RB - 1 and u == 1)
             else:
                 if b == 0:
@@ -395,7 +411,7 @@ def tile_list_canteen_menu_rotation_kernel(
 
         def finish(half, k, srcs, staged):
             for c in (2 * k, 2 * k + 1):
-                if half == 1 and c % 2 == 0:
+                if half == 1 and c in (0, 2, 6, 7):
                     nc.vector.tensor_scalar(staged[:, c, :], srcs[c], slot_sb[:, c : c + 1], None, ALU.add)
                 else:
                     nc.scalar.activation(staged[:, c, :], srcs[c], ACT.Identity, bias=slot_sb[:, c : c + 1], scale=1.0)
@@ -409,7 +425,10 @@ def tile_list_canteen_menu_rotation_kernel(
         z01 = make_z(0, 1)
         quant_z(0, 0, z00, nc.scalar.copy)
         quant_z(0, 1, z01, nc.scalar.copy)
-        quant_page(1, page_woven[1])
+        weave_page(1, 3)
+        quant_page(1, 0, 2)
+        quant_page(1, 2, 3)
+        quant_page(1, 3, 4)
         for b in range(RB):
             srcs = [out_pass(0, c, b) for c in range(T2 // P)]
         staged = [slab("staged_%d" % half, [P, T2 // P, HALF], F32) for half in range(2)]

from contextlib import ExitStack

import concourse.mybir as mybir

K, T, S, H, T2, NP = 1536, 2048, 512, 1024, 1024, 512
FLOPS = 2 * K * H * S + 2 * H * H * NP + 2 * H * T2 * NP

F32 = mybir.dt.float32
BF16 = mybir.dt.bfloat16
I32 = mybir.dt.int32
U32 = mybir.dt.uint32
U16 = mybir.dt.uint16
U8 = mybir.dt.uint8
FP8X4 = mybir.dt.float8_e4m3fn_x4
FP4X4 = mybir.dt.float4_e2m1fn_x4
ALU = mybir.AluOpType
ACT = mybir.ActivationFunctionType

P = 128
PACK = 4
KP = P * PACK
KA = K // KP
RB = H // KP
HALF = NP // 2


def tile_list_canteen_menu_rotation_kernel(
    tc, tab_words, tab_scales, offs, w1, resid, page0, wgs, offs2, offs3, w4_words, w4_scales, least, gain, slot, out
):
    nc = tc.nc
    with ExitStack() as ctx:
        keep = ctx.enter_context(tc.tile_pool(name="keep", bufs=1))
        ring = ctx.enter_context(tc.tile_pool(name="ring", bufs=1))
        psum = ctx.enter_context(tc.psum_pool(name="psum", bufs=1))

        def held(name, shape, dtype):
            return keep.tile(shape, dtype, name=name, align_bytes=64)

        def slab(name, shape, dtype):
            return ring.tile(shape, dtype, name=name, tag="slab", bufs=7, align_bytes=64)

        def bank(name, tag):
            return psum.tile([P, 512], F32, name=name, tag=tag, bufs=4 if tag == "b" else 2)

        idx = held("idx", [P, S // 16], U16)
        idx2 = held("idx2", [P, S // 16], U16)
        idx3 = held("idx3", [P, NP // 16], U16)

        tab_sc = held("tab_sc", [P, T], U8)
        w4_raw = held("w4_raw", [P, RB, 2 * H], U8)
        w4_sc_raw = ring.tile([P, RB, H], U8, name="w4_sc_raw", tag="early_sc", bufs=1, align_bytes=64)
        nc.vector.memset(tab_sc[:].bitcast(I32), 0)
        nc.vector.memset(w4_sc_raw[:].rearrange("p a n -> p (a n)").bitcast(I32), 0)

        def load_w1(b, a):
            if (b, a) == (RB - 1, KA - 1):
                raw = ring.tile([P, PACK, KP], F32, name="w1_raw_last", tag="last_raw", bufs=1, align_bytes=64)
            else:
                raw = slab("w1_raw_%d_%d" % (b, a), [P, PACK, KP], F32)
            src = w1[a * KP : (a + 1) * KP, b * KP : (b + 1) * KP].rearrange("(p i) c -> p i c", i=PACK)
            nc.sync.dma_start(out=raw[:], in_=src)
            return raw

        def load_tab(a):
            words = slab("tab_%d" % a, [P, T], I32)
            nc.sync.dma_start(out=words[:], in_=tab_words[a].rearrange("p t i -> p (t i)").bitcast(I32))
            return words

        resid_rows = resid.rearrange("(b p t) j -> b p t j", b=RB, t=PACK)
        page_rows = page0.rearrange("(b p t) m -> b t p m", b=RB, t=PACK)
        res = [held("res_%d" % i, [P, S], F32) for i in range(RB * PACK)]

        def load_res(i):
            nc.sync.dma_start(out=res[i][:], in_=resid_rows[i // PACK, :, i % PACK, :])

        page = [held("page_%d" % i, [P, T2], F32) for i in range(RB * PACK - 1)]

        def load_page(i):
            nc.sync.dma_start(out=page[i][:], in_=page_rows[i // PACK, i % PACK])

        nc.sync.dma_start(out=w4_raw[:].bitcast(I32), in_=w4_words.rearrange("a p c -> p a c").bitcast(I32))
        w1_raw = {}
        tab = []
        w1_raw[0, 0] = load_w1(0, 0)
        tab.append(load_tab(0))
        nc.sync.dma_start(idx[:], offs)
        for q in range(4):
            nc.gpsimd.dma_start(
                out=tab_sc[32 * q : 32 * q + 4 * KA, :].bitcast(I32),
                in_=tab_scales[:, 4 * q : 4 * q + 4, :].bitcast(I32),
            )
        for q in range(4):
            nc.sync.dma_start(
                out=w4_sc_raw[32 * q : 32 * q + 4, :, :].bitcast(I32),
                in_=w4_scales[:, 4 * q : 4 * q + 4, :].rearrange("a r n -> r a n").bitcast(I32),
            )
        w1_raw[0, 1] = load_w1(0, 1)
        w1_raw[0, 2] = load_w1(0, 2)
        tab.append(load_tab(1))
        wg_first = held("wg_first", [P, S], F32)
        wg_mid = held("wg_mid", [P, 2, S], F32)
        wg_last = held("wg_last", [P, S], F32)
        wg_rows = wgs.rearrange("(q t) j -> q t j", t=PACK)
        tab.append(load_tab(2))
        load_res(0)
        for q in range(4):
            nc.sync.dma_start(out=wg_first[32 * q : 32 * q + 32, :], in_=wg_rows[:, 0, :])
        nc.sync.dma_start(idx2[:], offs2)
        load_page(0)
        load_res(1)
        nc.sync.dma_start(idx3[:], offs3)
        for q in range(4):
            nc.sync.dma_start(out=wg_mid[32 * q : 32 * q + 32, :, :], in_=wg_rows[:, 1:3, :])
        load_page(1)
        load_res(2)
        w1_raw[1, 0] = load_w1(1, 0)
        load_page(2)
        load_res(3)
        w1_raw[1, 1] = load_w1(1, 1)
        for q in range(4):
            nc.sync.dma_start(out=wg_last[32 * q : 32 * q + 32, :], in_=wg_rows[:, 3, :])
        w1_raw[1, 2] = load_w1(1, 2)
        load_res(PACK)
        load_page(PACK - 1)
        for i in range(PACK, RB * PACK - 1):
            load_page(i)
            load_res(i + 1)
        least_sb = held("least_sb", [P, RB, PACK], F32)
        gain_sb = held("gain_sb", [P, RB, PACK], F32)
        slot_sb = held("slot_sb", [P, T2 // P], F32)
        nc.sync.dma_start(out=least_sb[:], in_=least.rearrange("(b p t) -> p b t", b=RB, t=PACK))
        nc.sync.dma_start(out=gain_sb[:], in_=gain.rearrange("(b p t) -> p b t", b=RB, t=PACK))
        with nc.allow_non_contiguous_dma(reason="one value of slot to a partition"):
            nc.sync.dma_start(out=slot_sb[:], in_=slot.rearrange("(c p) -> p c", p=P))

        def wg(t):
            return (wg_first[:], wg_mid[:, 0, :], wg_mid[:, 1, :], wg_last[:])[t]

        w4 = held("w4", [P, RB, 2 * H], U8)
        w4_sc = held("w4_sc", [P, RB, H], U8)
        for a in range(RB):
            nc.vector.tensor_copy(
                out=w4[:, a, :].bitcast(U16).rearrange("p (b t m) -> p b t m", b=RB, t=PACK),
                in_=w4_raw[:, a, :].bitcast(U16).rearrange("p (b m t) -> p b t m", b=RB, t=PACK),
            )
        nc.vector.tensor_copy(
            out=w4_sc[:].rearrange("p a (b t m) -> p (a b) t m", b=RB, t=PACK),
            in_=w4_sc_raw[:].rearrange("p a (b m t) -> p (a b) t m", b=RB, t=PACK),
        )

        v_sc = ring.tile([P, S], U8, name="v_sc", tag="early_sc", bufs=1, align_bytes=64)
        v = [held("v_%d" % a, [P, S], U32) for a in range(KA)]
        w1_codes = {}
        w1_sc = {}

        def gather_tab(a):
            nc.vector.tensor_copy(v[a][:], tab[a][:].bitcast(U32).indirect(idx[:]))

        def quant_w1(b, a, split):
            staged = ring.tile([P, PACK * KP], BF16, name="w1_bf_%d_%d" % (b, a), tag="w1_bf", bufs=3, align_bytes=64)
            dst = staged[:].rearrange("p (t m i) -> p m t i", t=PACK, i=PACK)
            src = w1_raw[b, a][:].rearrange("p i (m t) -> p m t i", t=PACK)
            if split:
                nc.scalar.copy(out=dst[:, 0:split], in_=src[:, 0:split])
                nc.vector.tensor_copy(out=dst[:, split:P], in_=src[:, split:P])
            else:
                nc.scalar.copy(out=dst, in_=src)
            w1_codes[b, a] = held("w1_codes_%d_%d" % (b, a), [P, KP], U32)
            w1_sc[b, a] = held("w1_sc_%d_%d" % (b, a), [P, KP], U8)
            nc.vector.quantize_mx(out=w1_codes[b, a][:].bitcast(FP8X4), scales=w1_sc[b, a][:], in_=staged[:])

        nc.vector.tensor_copy(v_sc[:], tab_sc[:].indirect(idx[:]))
        gather_tab(0)
        quant_w1(0, 0, 0)
        quant_w1(0, 1, 0)
        gather_tab(1)
        quant_w1(0, 2, 96)
        for half in range(2):
            cols = slice(half * HALF, (half + 1) * HALF)
            nc.vector.tensor_copy(
                v[KA - 1][:, cols], tab[KA - 1][:].bitcast(U32).indirect(idx[:, half * 16 : (half + 1) * 16])
            )

        h_bank = {}

        def h_pass(i, a):
            b, t = divmod(i, PACK)
            if a == 0:
                h_bank[i] = bank("h_bank_%d" % i, "a")
            cols = slice(t * P, (t + 1) * P)
            nc.tensor.matmul_mx(
                out=h_bank[i][:],
                lhsT=w1_codes[b, a][:, cols].bitcast(FP8X4),
                lhsT_scale=w1_sc[b, a][:, cols],
                rhs=v[a][:].bitcast(FP8X4),
                rhs_scale=v_sc[4 * a : P, :],
                start=(a == 0),
                stop=(a == KA - 1),
            )

        h_first = [bank("h_first_%d" % half, "a") for half in range(2)]
        for a in range(KA):
            for half in range(2):
                cols = slice(half * HALF, (half + 1) * HALF)
                nc.tensor.matmul_mx(
                    out=h_first[half][:, 0:HALF],
                    lhsT=w1_codes[0, a][:, 0:P].bitcast(FP8X4),
                    lhsT_scale=w1_sc[0, a][:, 0:P],
                    rhs=v[a][:, cols].bitcast(FP8X4),
                    rhs_scale=v_sc[4 * a : P, cols],
                    start=(a == 0),
                    stop=(a == KA - 1),
                )
            for i in range(1, PACK):
                h_pass(i, a)

        x_planes = [held("x_planes_%d" % b, [P, PACK, NP], F32) for b in range(RB)]
        x_codes = {1: held("x_codes_1", [P, NP], U32)}
        x_sc = [held("x_sc_%d" % b, [P, NP], U8) for b in range(RB)]
        pg_codes = [held("pg_codes_%d" % b, [P, T2], U32) for b in range(RB)]
        pg_sc = {1: held("pg_sc_1", [P, T2], U8)}

        def woven(name):
            return ring.tile([P, PACK * HALF], BF16, name=name, tag="woven", bufs=4, align_bytes=64)

        def weave(copy, dst, planes):
            copy(
                out=dst.rearrange("p (c i t) -> p c t i", i=4, t=PACK),
                in_=planes.rearrange("p t (c i) -> p c t i", i=4),
            )

        x_woven = {}

        def weave_x(b, half, copy):
            if (b, half) == (1, 0):
                dst = ring.tile([P, PACK * HALF], BF16, name="x_woven_1_0", tag="x_first", bufs=1, align_bytes=64)
            else:
                dst = woven("x_woven_%d_%d" % (b, half))
            planes = x_planes[b][:, :, half * HALF : (half + 1) * HALF]
            if copy is None:
                weave(nc.scalar.copy, dst[:, 0 : PACK * 64], planes[:, :, 0:64])
                weave(nc.vector.tensor_copy, dst[:, PACK * 64 : PACK * HALF], planes[:, :, 64:HALF])
            else:
                weave(copy, dst[:], planes)
            x_woven[b, half] = dst

        def quant_x(b, half):
            cols = slice(half * HALF, (half + 1) * HALF)
            dst = x_woven[b, half]
            nc.vector.quantize_mx(out=x_codes[b][:, cols].bitcast(FP8X4), scales=x_sc[b][:, cols], in_=dst[:])

        page_woven = {}
        PART = T2 // 4

        def weave_page(b, part):
            if part == 0:
                page_woven[b] = slab("pg_woven_%d" % b, [P, PACK * T2], BF16)
            weave(
                nc.scalar.copy,
                page_woven[b][:, PACK * PART * part : PACK * PART * (part + 1)],
                page_planes[b][:, :, PART * part : PART * (part + 1)],
            )

        def quant_page(b, lo, hi):
            nc.vector.quantize_mx(
                out=pg_codes[b][:, PART * lo : PART * hi].bitcast(FP8X4),
                scales=pg_sc[b][:, PART * lo : PART * hi],
                in_=page_woven[b][:, PACK * PART * lo : PACK * PART * hi],
            )

        y_bank = {}

        def y_pass(half, k, a):
            if a == 0:
                y_bank[half, k] = bank("y_bank_%d_%d" % (half, k), "b" if half == 0 else ("c" if k < 2 else "a"))
            for u in range(2):
                n = 2 * k + u
                for c in range(2):
                    cols = slice(half * HALF + c * P, half * HALF + (c + 1) * P)
                    nc.tensor.matmul_mx(
                        out=y_bank[half, k][:, u * HALF + c * P : u * HALF + (c + 1) * P],
                        lhsT=w4[:, a, 2 * P * n : 2 * P * (n + 1)].bitcast(FP4X4),
                        lhsT_scale=w4_sc[:, a, P * n : P * (n + 1)],
                        rhs=x_codes[a][:, cols].bitcast(FP8X4),
                        rhs_scale=x_sc[a][:, cols],
                        start=(a == 0 and u == 0 and c == 0),
                        stop=(a == RB - 1 and u == 1 and c == 1),
                    )

        h = {}
        page_planes = []

        def add_resid(i):
            if i == RB * PACK - 1:
                h[i] = ring.tile([P, S], F32, name="h_%d" % i, tag="h_last", bufs=1, align_bytes=64)
            else:
                h[i] = ring.tile([P, S], F32, name="h_%d" % i, tag="h", bufs=2)
            nc.vector.tensor_tensor(h[i][:], h_bank[i][:], res[i][:], ALU.add)

        for half in range(2):
            cols = slice(half * HALF, (half + 1) * HALF)
            part = ring.tile([P, HALF], F32, name="h_first_%d" % half, tag="h", bufs=2)
            nc.vector.tensor_tensor(part[:], h_first[half][:, 0:HALF], res[0][:, cols], ALU.add)
            nc.vector.tensor_tensor(
                page[0][:].indirect(idx2[:, half * 16 : (half + 1) * 16]), part[:], wg_first[:, cols], ALU.mult
            )
        for i in range(RB * PACK):
            b, t = divmod(i, PACK)
            if i > 0:
                nc.vector.tensor_tensor(page[i][:].indirect(idx2[:]), h[i][:], wg(t), ALU.mult)
            if i < KA:
                quant_w1(1, i, 0)
            if i == KA - 1:
                for a in range(KA):
                    for i2 in range(PACK, 2 * PACK):
                        h_pass(i2, a)
            if i + 1 < RB * PACK:
                add_resid(i + 1)
            if i == RB * PACK - 1:
                x_codes[0] = ring.tile([P, NP], U32, name="x_codes_0", tag="h_last", bufs=1, align_bytes=64)
                quant_x(0, 0)
                for k in range(4):
                    y_pass(0, k, 0)
            nc.vector.tensor_copy(x_planes[b][:, t, :], page[i][:].indirect(idx3[:]))
            if i == PACK:
                page_planes.append(slab("planes_1", [P, PACK, T2], BF16))
            if i == KA - 1:
                page_planes.append(ring.tile([P, PACK, T2], BF16, name="planes_0", tag="last_raw", bufs=1, align_bytes=64))
                for i2 in range(i):
                    nc.scalar.copy(out=page_planes[0][:, i2, :], in_=page[i2][:])
            if i >= KA - 1:
                nc.scalar.copy(out=page_planes[b][:, t, :], in_=page[i][:])
            if i == PACK - 1:
                weave_x(0, 0, nc.scalar.copy)
                weave_x(0, 1, nc.scalar.copy)
                for part in range(4):
                    weave_page(0, part)
                page.append(ring.tile([P, T2], F32, name="page_last", tag="last_raw", bufs=1, align_bytes=64))
                load_page(RB * PACK - 1)
        weave_x(1, 0, None)
        quant_x(0, 1)
        quant_x(1, 0)
        for k in range(4):
            y_pass(0, k, 1)
        weave_x(1, 1, nc.scalar.copy)
        for part in range(3):
            weave_page(1, part)
        pg_sc[0] = ring.tile([P, T2], U8, name="pg_sc_0", tag="x_first", bufs=1, align_bytes=64)
        quant_page(0, 0, 2)
        quant_page(0, 2, 4)
        quant_x(1, 1)
        for a in range(RB):
            for k in range(4):
                y_pass(1, k, a)

        z_codes = {}
        z_sc = {}

        def make_z(half, b):
            planes = ring.tile([P, PACK, HALF], BF16, name="z_planes_%d_%d" % (half, b), tag="z_planes", bufs=4)
            for t in range(PACK):
                k, u = divmod(PACK * b + t, 2)
                nc.vector.tensor_scalar(
                    planes[:, t, :],
                    y_bank[half, k][:, u * HALF : (u + 1) * HALF],
                    least_sb[:, b, t : t + 1],
                    gain_sb[:, b, t : t + 1],
                    ALU.max,
                    ALU.mult,
                )
            return planes

        def quant_z(half, b, planes, copy):
            dst = woven("z_woven_%d_%d" % (half, b))
            if copy is None:
                cut = 192
                weave(nc.scalar.copy, dst[:, 0 : PACK * cut], planes[:, :, 0:cut])
                weave(nc.vector.tensor_copy, dst[:, PACK * cut : PACK * HALF], planes[:, :, cut:HALF])
            else:
                weave(copy, dst[:], planes[:])
            z_codes[half, b] = held("z_codes_%d_%d" % (half, b), [P, HALF], U32)
            z_sc[half, b] = held("z_sc_%d_%d" % (half, b), [P, HALF], U8)
            nc.vector.quantize_mx(out=z_codes[half, b][:].bitcast(FP8X4), scales=z_sc[half, b][:], in_=dst[:])

        o_bank = {}

        def out_pass(half, c, b):
            k, u = divmod(c, 2)
            if half == 0 or k == 3:
                if b == 0 and u == 0:
                    o_bank[half, c] = bank("o_bank_%d_%d" % (half, c), "b")
                    o_bank[half, c + 1] = o_bank[half, c]
                dst = o_bank[half, c][:, u * HALF : (u + 1) * HALF]
                first, last = (b == 0 and u == 0), (b == RB - 1 and u == 1)
            else:
                if b == 0:
                    o_bank[1, c] = bank("o_bank_1_%d" % c, ("c", "c", "a", "a", "b", "b", "b", "b")[c])
                dst = o_bank[1, c][:, 0:HALF]
                first, last = b == 0, b == RB - 1
            cols = slice(c * P, (c + 1) * P)
            nc.tensor.matmul_mx(
                out=dst,
                lhsT=pg_codes[b][:, cols].bitcast(FP8X4),
                lhsT_scale=pg_sc[b][:, cols],
                rhs=z_codes[half, b][:].bitcast(FP8X4),
                rhs_scale=z_sc[half, b][:],
                start=first,
                stop=last,
            )
            return dst

        def finish(half, k, srcs, staged):
            for c in (2 * k, 2 * k + 1):
                if half == 1 and c in (0, 2, 6, 7):
                    nc.vector.tensor_scalar(staged[:, c, :], srcs[c], slot_sb[:, c : c + 1], None, ALU.add)
                else:
                    nc.scalar.activation(staged[:, c, :], srcs[c], ACT.Identity, bias=slot_sb[:, c : c + 1], scale=1.0)
                if half == 1:
                    nc.sync.dma_start(out=out[c * P : (c + 1) * P, HALF:NP], in_=staged[:, c, :])
            if half == 0:
                rows = out[2 * k * P : (2 * k + 2) * P, 0:HALF]
                nc.sync.dma_start(out=rows.rearrange("(u p) j -> p u j", p=P), in_=staged[:, 2 * k : 2 * k + 2, :])

        z00 = make_z(0, 0)
        z01 = make_z(0, 1)
        quant_z(0, 0, z00, nc.scalar.copy)
        quant_z(0, 1, z01, nc.scalar.copy)
        weave_page(1, 3)
        quant_page(1, 0, 2)
        quant_page(1, 2, 3)
        quant_page(1, 3, 4)
        for b in range(RB):
            srcs = [out_pass(0, c, b) for c in range(T2 // P)]
        staged = [slab("staged_%d" % half, [P, T2 // P, HALF], F32) for half in range(2)]
        z10 = make_z(1, 0)
        quant_z(1, 0, z10, None)
        for k in range(4):
            finish(0, k, srcs, staged[0])
        z11 = make_z(1, 1)
        for c in range(T2 // P):
            out_pass(1, c, 0)
        quant_z(1, 1, z11, nc.vector.tensor_copy)
        srcs = [out_pass(1, c, 1) for c in range(T2 // P)]
        for k in range(4):
            finish(1, k, srcs, staged[1])
